import numpy as np, ml_dtypes
CORES = [9,10,11,14,17,18,19,22,49,50,51,54]
N = 12
DEG, TK = 3, 512
MASK = [[11,0,1],[0,1,2],[1,2,3],[2,3,4],[3,4,5],[4,5,6],[5,6,7],[6,7,8],[7,8,9],[8,9,10],[9,10,11],[10,11,0]]
def setup_inputs(rng):
    return {"x": rng.standard_normal((N, 128, TK), dtype=np.float32).astype(ml_dtypes.bfloat16), "w": rng.standard_normal((N, 128, DEG * 128), dtype=np.float32).astype(ml_dtypes.bfloat16)}
def setup_inputs_big(rng):
    d = setup_inputs(rng)
    for k in ("x", "w"): d[k] = (d[k].astype(np.float32) * 1024.0).astype(d[k].dtype)
    return d
def setup_inputs_small(rng):
    d = setup_inputs(rng)
    for k in ("x", "w"): d[k] = (d[k].astype(np.float32) * (1 / 1024.0)).astype(d[k].dtype)
    return d
def setup_inputs_apart(rng):
    d = setup_inputs(rng)
    f = (10.0 ** rng.permutation(np.linspace(-1.5, 1.5, N))).astype(np.float32).reshape(N, 1, 1)
    for k in ("x", "w"): d[k] = (d[k].astype(np.float32) * f).astype(d[k].dtype)
    return d
def reference(x, w):
    X, W = x.astype(np.float64), w.astype(np.float64)
    y = np.zeros((N, 128, TK))
    for r in range(N):
        for i, j in enumerate(MASK[r]):
            y[r] += W[r][:, 128 * i:128 * i + 128].T @ X[j]
    return {"y": y.astype(ml_dtypes.bfloat16 if x.dtype != np.float64 else np.float64)}

@@ -1,0 +1,104 @@
+TK = 512
+PW = 128
+NE = 8
+
+SCRATCH = {
+    "xs": ("sbuf", [128, 3 * TK], "bfloat16"),
+    "ws": ("sbuf", [128, 3 * PW], "bfloat16"),
+    "yb": ("sbuf", [128, TK], "bfloat16"),
+    "ps": ("psum", [128, TK], "float32"),
+}
+SEMAPHORES = ["xl", "wl", "a0", "a1", "a2", "sent", "mm", "cp", "st"]
+
+
+def _routes(cores, tab, topo):
+    out = []
+    for r, row in enumerate(tab):
+        for i, j in enumerate(row):
+            if j == r:
+                continue
+            via = None
+            if not topo.may_write(cores[j], cores[r]):
+                for k, krow in enumerate(tab):
+                    if (k != j and k != r and j in krow and topo.chip(cores[k]) == topo.chip(cores[j])
+                            and topo.may_write(cores[j], cores[k]) and topo.may_write(cores[k], cores[r])):
+                        via = k
+                        break
+                if via is None:
+                    raise ValueError("no rank can pass x%d on to rank %d" % (j, r))
+            out.append((j, r, i, via))
+    return out
+
+
+def _writes(rank, cores, tab, topo, routes):
+    own = tab[rank].index(rank)
+    passers = [via for (j, r, i, via) in routes if j == rank and via is not None]
+    first = [(0 if r in passers else 1, 0 if topo.chip(cores[r]) != topo.chip(cores[rank]) else 1, r, i)
+             for (j, r, i, via) in routes if j == rank and via is None]
+    mine = [(own, r, i) for (_, _, r, i) in sorted(first)]
+    onward = [(tab[rank].index(j), r, i) for (j, r, i, via) in routes if via == rank]
+    return mine, onward
+
+
+def _engines(rank, cores, tab, topo, routes):
+    mine, onward = _writes(rank, cores, tab, topo, routes)
+    common = None
+    for (_, r, _) in mine + onward:
+        m = topo.mask(cores[rank], cores[r])
+        common = m if common is None else common & m
+    bits = [e for e in range(common.bit_length()) if (common >> e) & 1][:NE]
+    return sum(1 << e for e in bits), len(bits)
+
+
+def rank_program(g, core, T, topo):
+    rank = T.rank_of(core)
+    if rank is None:
+        return
+    cores = list(T.cores)
+    tab = T.tables["MASK"]
+    sem = T.sem
+    routes = _routes(cores, tab, topo)
+    own = tab[rank].index(rank)
+
+    def slot(i):
+        return T.xs[:, i * TK:(i + 1) * TK]
+
+    lands = {}
+    for (j, r, i, via) in routes:
+        if r == rank:
+            writer = j if via is None else via
+            late = 2 if via is not None else (1 if topo.chip(cores[j]) != topo.chip(core) else 0)
+            lands[i] = (_engines(writer, cores, tab, topo, routes)[1], late)
+
+    g.sync.dma_start(slot(own), T.x[:]).then_inc(sem.xl, 16)
+    g.sync.dma_start(T.ws[:], T.w[:]).then_inc(sem.wl, 16)
+
+    mine, onward = _writes(rank, cores, tab, topo, routes)
+    emask, ne = _engines(rank, cores, tab, topo, routes)
+    g.wait_ge(sem.xl, 16)
+    left = 0
+    for n, (s, r, i) in enumerate(mine + onward):
+        if n >= len(mine):
+            g.wait_ge(sem["a%d" % s], lands[s][0])
+        rid, pid, _ = topo.addr(cores[r])
+        g.remote_dma(out_ap=slot(i), in_ap=slot(s), remote_sem=sem["a%d" % i], local_sem=sem.sent,
+                     pid=pid, routing_id=rid, dma_engine_mask=emask)
+        left += ne
+    g.wait_ge(sem.sent, left)
+
+    order = [own] + sorted(lands, key=lambda i: (lands[i][1], i))
+    g.tensor.wait_ge(sem.wl, 16)
+    g.tensor.wait_ge(sem.xl, 16)
+    for n, i in enumerate(order):
+        if i != own:
+            g.tensor.wait_ge(sem["a%d" % i], lands[i][0])
+        mm = g.tensor.matmul(T.ps[:], T.ws[:, i * PW:(i + 1) * PW], slot(i), start=(n == 0), stop=(n == len(order) - 1))
+        if n == len(order) - 1:
+            mm.then_inc(sem.mm, 1)
+
+    g.vector.wait_ge(sem.mm, 1)
+    g.vector.tensor_copy(T.yb[:], T.ps[:]).then_inc(sem.cp, 1)
+
+    g.sync.wait_ge(sem.cp, 1)
+    g.sync.dma_start(T.y[:], T.yb[:]).then_inc(sem.st, 16)
+    g.sync.wait_ge(sem.st, 16)

@@ -1,53 +1,101 @@
+from concourse.bass import DstId, RemoteDMATransfer
+
 TK = 512
+H = TK // 2
 PW = 128
-NE = 8
 
 SCRATCH = {
     "xs": ("sbuf", [128, 3 * TK], "bfloat16"),
+    "rb": ("sbuf", [128, H], "bfloat16"),
     "ws": ("sbuf", [128, 3 * PW], "bfloat16"),
     "yb": ("sbuf", [128, TK], "bfloat16"),
-    "ps": ("psum", [128, TK], "float32"),
+    "ps0": ("psum", [128, TK], "float32"),
+    "ps1": ("psum", [128, TK], "float32"),
 }
-SEMAPHORES = ["xl", "wl", "a0", "a1", "a2", "sent", "mm", "cp", "st"]
+SEMAPHORES = ["xl", "wl", "a00", "a01", "a10", "a11", "a20", "a21", "rl", "sent",
+              "mm0", "mm1", "cp0", "cp1", "st0", "st1"]
 
 
-def _routes(cores, tab, topo):
-    out = []
-    for r, row in enumerate(tab):
-        for i, j in enumerate(row):
-            if j == r:
-                continue
-            via = None
-            if not topo.may_write(cores[j], cores[r]):
-                for k, krow in enumerate(tab):
-                    if (k != j and k != r and j in krow and topo.chip(cores[k]) == topo.chip(cores[j])
-                            and topo.may_write(cores[j], cores[k]) and topo.may_write(cores[k], cores[r])):
-                        via = k
-                        break
-                if via is None:
-                    raise ValueError("no rank can pass x%d on to rank %d" % (j, r))
-            out.append((j, r, i, via))
-    return out
+def _deal(topo, src, dsts):
+    masks = [topo.mask(src, d) for d in dsts]
+    union = 0
+    for m in masks:
+        union |= m
+    free = [e for e in range(union.bit_length()) if (union >> e) & 1]
+    per = 1
+    while per * 2 * len(dsts) <= len(free):
+        per *= 2
+    got = [None] * len(dsts)
+    wide = [n for n in range(len(dsts)) if masks[n] == union]
+    for n in range(len(dsts)):
+        if masks[n] != union:
+            got[n] = [e for e in free if (masks[n] >> e) & 1][:per]
+            free = [e for e in free if e not in got[n]]
+    for k, n in enumerate(wide):
+        got[n] = free[k::len(wide)][:per]
+    return got
 
 
-def _writes(rank, cores, tab, topo, routes):
-    own = tab[rank].index(rank)
-    passers = [via for (j, r, i, via) in routes if j == rank and via is not None]
-    first = [(0 if r in passers else 1, 0 if topo.chip(cores[r]) != topo.chip(cores[rank]) else 1, r, i)
-             for (j, r, i, via) in routes if j == rank and via is None]
-    mine = [(own, r, i) for (_, _, r, i) in sorted(first)]
-    onward = [(tab[rank].index(j), r, i) for (j, r, i, via) in routes if via == rank]
-    return mine, onward
+def _plan(cores, tab, topo):
+    n = len(cores)
+    calls = {r: [] for r in range(n)}
+    onward = {r: [] for r in range(n)}
+    lands = {r: [] for r in range(n)}
+    adds = {}
 
+    def call(rank, wait, items):
+        eng = _deal(topo, cores[rank], [cores[it[0]] for it in items])
+        trs = []
+        for it, e in zip(items, eng):
+            trs.append(it + (e,))
+            adds[(it[0], it[4])] = adds.get((it[0], it[4]), 0) + len(e)
+        return (wait, trs)
 
-def _engines(rank, cores, tab, topo, routes):
-    mine, onward = _writes(rank, cores, tab, topo, routes)
-    common = None
-    for (_, r, _) in mine + onward:
-        m = topo.mask(cores[rank], cores[r])
-        common = m if common is None else common & m
-    bits = [e for e in range(common.bit_length()) if (common >> e) & 1][:NE]
-    return sum(1 << e for e in bits), len(bits)
+    for j in range(n):
+        own = tab[j].index(j)
+        readers = [(r, tab[r].index(j)) for r in range(n) if r != j and j in tab[r]]
+        direct = [(r, i) for (r, i) in readers if topo.may_write(cores[j], cores[r])]
+        blocked = [(r, i) for (r, i) in readers if not topo.may_write(cores[j], cores[r])]
+        if not blocked:
+            items = []
+            for (r, i) in direct:
+                items.append((r, ("xs", own * TK), ("xs", i * TK), TK, "a%d0" % i))
+                lands[r].append((i, None, "a%d0" % i, 2 if topo.chip(cores[r]) != topo.chip(cores[j]) else 0))
+            calls[j].append(call(j, None, items))
+            continue
+        if len(blocked) > 1:
+            raise ValueError("x%d has more than one reader that its core may not write to" % j)
+        r, i = blocked[0]
+        slot_of = dict(direct)
+        cand = [k for k in range(n) if k != j and k != r and topo.chip(cores[k]) == topo.chip(cores[j])
+                and topo.may_write(cores[j], cores[k]) and topo.may_write(cores[k], cores[r])]
+        ka = sorted(cand, key=lambda k: (k not in slot_of, topo.die(cores[k]) != topo.die(cores[j]), k))[0]
+        kb = sorted([k for k in cand if k != ka],
+                    key=lambda k: (topo.die(cores[k]) == topo.die(cores[ka]), k not in slot_of, k))[0]
+        first, given = [], []
+        for h, k in enumerate((ka, kb)):
+            if k in slot_of:
+                at, s = ("xs", slot_of[k] * TK + h * H), "a%d%d" % (slot_of[k], h)
+                lands[k].append((slot_of[k], h, s, 1))
+                given.append((k, h))
+            else:
+                at, s = ("rb", 0), "rl"
+            first.append((k, ("xs", own * TK + h * H), at, H, s))
+            onward[k].append((s, [(r, at, ("xs", i * TK + h * H), H, "a%d%d" % (i, h))]))
+            lands[r].append((i, h, "a%d%d" % (i, h), 3))
+        calls[j].append(call(j, None, first))
+        rest = []
+        for (k, ik) in direct:
+            for h in range(2):
+                if (k, h) not in given:
+                    rest.append((k, ("xs", own * TK + h * H), ("xs", ik * TK + h * H), H, "a%d%d" % (ik, h)))
+                    lands[k].append((ik, h, "a%d%d" % (ik, h), 1))
+        if rest:
+            calls[j].append(call(j, None, rest))
+    for k in range(n):
+        for (s, items) in onward[k]:
+            calls[k].append(call(k, s, items))
+    return calls, lands, adds
 
 
 def rank_program(g, core, T, topo):
@@ -57,48 +105,53 @@ def rank_program(g, core, T, topo):
     cores = list(T.cores)
     tab = T.tables["MASK"]
     sem = T.sem
-    routes = _routes(cores, tab, topo)
+    calls, lands, adds = _plan(cores, tab, topo)
     own = tab[rank].index(rank)
 
-    def slot(i):
-        return T.xs[:, i * TK:(i + 1) * TK]
+    def cols(where, width):
+        return T[where[0]][:, where[1]:where[1] + width]
 
-    lands = {}
-    for (j, r, i, via) in routes:
-        if r == rank:
-            writer = j if via is None else via
-            late = 2 if via is not None else (1 if topo.chip(cores[j]) != topo.chip(core) else 0)
-            lands[i] = (_engines(writer, cores, tab, topo, routes)[1], late)
-
-    g.sync.dma_start(slot(own), T.x[:]).then_inc(sem.xl, 16)
+    g.sync.dma_start(cols(("xs", own * TK), TK), T.x[:]).then_inc(sem.xl, 16)
     g.sync.dma_start(T.ws[:], T.w[:]).then_inc(sem.wl, 16)
 
-    mine, onward = _writes(rank, cores, tab, topo, routes)
-    emask, ne = _engines(rank, cores, tab, topo, routes)
     g.wait_ge(sem.xl, 16)
     left = 0
-    for n, (s, r, i) in enumerate(mine + onward):
-        if n >= len(mine):
-            g.wait_ge(sem["a%d" % s], lands[s][0])
-        rid, pid, _ = topo.addr(cores[r])
-        g.remote_dma(out_ap=slot(i), in_ap=slot(s), remote_sem=sem["a%d" % i], local_sem=sem.sent,
-                     pid=pid, routing_id=rid, dma_engine_mask=emask)
-        left += ne
+    for (wait, trs) in calls[rank]:
+        if wait is not None:
+            g.wait_ge(sem[wait], adds[(rank, wait)])
+        fused = []
+        for (r, here, there, width, s, eng) in trs:
+            rid, pid, _ = topo.addr(cores[r])
+            fused.append(RemoteDMATransfer(dst_ids=[DstId(rid=rid, pnc=pid)], dma_engine_mask=sum(1 << e for e in eng),
+                                           remote_sem=sem[s], src=cols(here, width), dst=cols(there, width)))
+            left += len(eng)
+        g.remote_dma_fused(fused, local_sem=sem.sent)
     g.wait_ge(sem.sent, left)
 
-    order = [own] + sorted(lands, key=lambda i: (lands[i][1], i))
+    steps = [(-1, own, 0, None), (-1, own, 1, None)]
+    for (i, h, s, late) in lands[rank]:
+        for hh in ((0, 1) if h is None else (h,)):
+            steps.append((late, i, hh, s))
+    steps.sort(key=lambda st: st[:3])
+    bank = (T.ps0, T.ps1)
+    todo = [sum(1 for st in steps if st[2] == h) for h in range(2)]
+    done = [0, 0]
+    waited = []
     g.tensor.wait_ge(sem.wl, 16)
     g.tensor.wait_ge(sem.xl, 16)
-    for n, i in enumerate(order):
-        if i != own:
-            g.tensor.wait_ge(sem["a%d" % i], lands[i][0])
-        mm = g.tensor.matmul(T.ps[:], T.ws[:, i * PW:(i + 1) * PW], slot(i), start=(n == 0), stop=(n == len(order) - 1))
-        if n == len(order) - 1:
-            mm.then_inc(sem.mm, 1)
+    for (late, i, h, s) in steps:
+        if s is not None and s not in waited:
+            g.tensor.wait_ge(sem[s], adds[(rank, s)])
+            waited.append(s)
+        done[h] += 1
+        mm = g.tensor.matmul(bank[h][:, 0:H], T.ws[:, i * PW:(i + 1) * PW], cols(("xs", i * TK + h * H), H),
+                             start=(done[h] == 1), stop=(done[h] == todo[h]))
+        if done[h] == todo[h]:
+            mm.then_inc(sem["mm%d" % h], 1)
 
-    g.vector.wait_ge(sem.mm, 1)
-    g.vector.tensor_copy(T.yb[:], T.ps[:]).then_inc(sem.cp, 1)
-
-    g.sync.wait_ge(sem.cp, 1)
-    g.sync.dma_start(T.y[:], T.yb[:]).then_inc(sem.st, 16)
-    g.sync.wait_ge(sem.st, 16)
+    for h, q in enumerate((g.sync, g.scalar)):
+        g.vector.wait_ge(sem["mm%d" % h], 1)
+        g.vector.tensor_copy(T.yb[:, h * H:(h + 1) * H], bank[h][:, 0:H]).then_inc(sem["cp%d" % h], 1)
+        q.wait_ge(sem["cp%d" % h], 1)
+        q.dma_start(T.y[:, h * H:(h + 1) * H], T.yb[:, h * H:(h + 1) * H]).then_inc(sem["st%d" % h], 16)
+        q.wait_ge(sem["st%d" % h], 16)

from concourse.bass import DstId, RemoteDMATransfer

TK = 512
H = TK // 2
PW = 128

SCRATCH = {
    "xs": ("sbuf", [128, 3 * TK], "bfloat16"),
    "rb": ("sbuf", [128, H], "bfloat16"),
    "ws": ("sbuf", [128, 3 * PW], "bfloat16"),
    "yb": ("sbuf", [128, TK], "bfloat16"),
    "ps0": ("psum", [128, TK], "float32"),
    "ps1": ("psum", [128, TK], "float32"),
}
SEMAPHORES = ["xl", "wl", "a00", "a01", "a10", "a11", "a20", "a21", "rl", "sent",
              "mm0", "mm1", "cp0", "cp1", "st0", "st1"]


def _deal(topo, src, dsts):
    masks = [topo.mask(src, d) for d in dsts]
    union = 0
    for m in masks:
        union |= m
    free = [e for e in range(union.bit_length()) if (union >> e) & 1]
    per = 1
    while per * 2 * len(dsts) <= len(free):
        per *= 2
    got = [None] * len(dsts)
    wide = [n for n in range(len(dsts)) if masks[n] == union]
    for n in range(len(dsts)):
        if masks[n] != union:
            got[n] = [e for e in free if (masks[n] >> e) & 1][:per]
            free = [e for e in free if e not in got[n]]
    for k, n in enumerate(wide):
        got[n] = free[k::len(wide)][:per]
    return got


def _plan(cores, tab, topo):
    n = len(cores)
    calls = {r: [] for r in range(n)}
    onward = {r: [] for r in range(n)}
    lands = {r: [] for r in range(n)}
    adds = {}

    def call(rank, wait, items):
        eng = _deal(topo, cores[rank], [cores[it[0]] for it in items])
        trs = []
        for it, e in zip(items, eng):
            trs.append(it + (e,))
            adds[(it[0], it[4])] = adds.get((it[0], it[4]), 0) + len(e)
        return (wait, trs)

    for j in range(n):
        own = tab[j].index(j)
        readers = [(r, tab[r].index(j)) for r in range(n) if r != j and j in tab[r]]
        direct = [(r, i) for (r, i) in readers if topo.may_write(cores[j], cores[r])]
        blocked = [(r, i) for (r, i) in readers if not topo.may_write(cores[j], cores[r])]
        if not blocked:
            items = []
            for (r, i) in direct:
                items.append((r, ("xs", own * TK), ("xs", i * TK), TK, "a%d0" % i))
                lands[r].append((i, None, "a%d0" % i, 2 if topo.chip(cores[r]) != topo.chip(cores[j]) else 0))
            calls[j].append(call(j, None, items))
            continue
        if len(blocked) > 1:
            raise ValueError("x%d has more than one reader that its core may not write to" % j)
        r, i = blocked[0]
        slot_of = dict(direct)
        cand = [k for k in range(n) if k != j and k != r and topo.chip(cores[k]) == topo.chip(cores[j])
                and topo.may_write(cores[j], cores[k]) and topo.may_write(cores[k], cores[r])]
        ka = sorted(cand, key=lambda k: (k not in slot_of, topo.die(cores[k]) != topo.die(cores[j]), k))[0]
        kb = sorted([k for k in cand if k != ka],
                    key=lambda k: (topo.die(cores[k]) == topo.die(cores[ka]), k not in slot_of, k))[0]
        first, given = [], []
        for h, k in enumerate((ka, kb)):
            if k in slot_of:
                at, s = ("xs", slot_of[k] * TK + h * H), "a%d%d" % (slot_of[k], h)
                lands[k].append((slot_of[k], h, s, 1))
                given.append((k, h))
            else:
                at, s = ("rb", 0), "rl"
            first.append((k, ("xs", own * TK + h * H), at, H, s))
            onward[k].append((s, [(r, at, ("xs", i * TK + h * H), H, "a%d%d" % (i, h))]))
            lands[r].append((i, h, "a%d%d" % (i, h), 3))
        calls[j].append(call(j, None, first))
        rest = []
        for (k, ik) in direct:
            for h in range(2):
                if (k, h) not in given:
                    rest.append((k, ("xs", own * TK + h * H), ("xs", ik * TK + h * H), H, "a%d%d" % (ik, h)))
                    lands[k].append((ik, h, "a%d%d" % (ik, h), 1))
        if rest:
            calls[j].append(call(j, None, rest))
    for k in range(n):
        for (s, items) in onward[k]:
            calls[k].append(call(k, s, items))
    return calls, lands, adds


def rank_program(g, core, T, topo):
    rank = T.rank_of(core)
    if rank is None:
        return
    cores = list(T.cores)
    tab = T.tables["MASK"]
    sem = T.sem
    calls, lands, adds = _plan(cores, tab, topo)
    own = tab[rank].index(rank)

    def cols(where, width):
        return T[where[0]][:, where[1]:where[1] + width]

    g.sync.dma_start(cols(("xs", own * TK), TK), T.x[:]).then_inc(sem.xl, 16)
    g.sync.dma_start(T.ws[:], T.w[:]).then_inc(sem.wl, 16)

    g.wait_ge(sem.xl, 16)
    left = 0
    for (wait, trs) in calls[rank]:
        if wait is not None:
            g.wait_ge(sem[wait], adds[(rank, wait)])
        fused = []
        for (r, here, there, width, s, eng) in trs:
            rid, pid, _ = topo.addr(cores[r])
            fused.append(RemoteDMATransfer(dst_ids=[DstId(rid=rid, pnc=pid)], dma_engine_mask=sum(1 << e for e in eng),
                                           remote_sem=sem[s], src=cols(here, width), dst=cols(there, width)))
            left += len(eng)
        g.remote_dma_fused(fused, local_sem=sem.sent)
    g.wait_ge(sem.sent, left)

    steps = [(-1, own, 0, None), (-1, own, 1, None)]
    for (i, h, s, late) in lands[rank]:
        for hh in ((0, 1) if h is None else (h,)):
            steps.append((late, i, hh, s))
    steps.sort(key=lambda st: st[:3])
    bank = (T.ps0, T.ps1)
    todo = [sum(1 for st in steps if st[2] == h) for h in range(2)]
    done = [0, 0]
    waited = []
    g.tensor.wait_ge(sem.wl, 16)
    g.tensor.wait_ge(sem.xl, 16)
    for (late, i, h, s) in steps:
        if s is not None and s not in waited:
            g.tensor.wait_ge(sem[s], adds[(rank, s)])
            waited.append(s)
        done[h] += 1
        mm = g.tensor.matmul(bank[h][:, 0:H], T.ws[:, i * PW:(i + 1) * PW], cols(("xs", i * TK + h * H), H),
                             start=(done[h] == 1), stop=(done[h] == todo[h]))
        if done[h] == todo[h]:
            mm.then_inc(sem["mm%d" % h], 1)

    for h, q in enumerate((g.sync, g.scalar)):
        g.vector.wait_ge(sem["mm%d" % h], 1)
        g.vector.tensor_copy(T.yb[:, h * H:(h + 1) * H], bank[h][:, 0:H]).then_inc(sem["cp%d" % h], 1)
        q.wait_ge(sem["cp%d" % h], 1)
        q.dma_start(T.y[:, h * H:(h + 1) * H], T.yb[:, h * H:(h + 1) * H]).then_inc(sem["st%d" % h], 16)
        q.wait_ge(sem["st%d" % h], 16)
